import numpy as np, ml_dtypes
CORES = [78,86,94,102,110,118]
N = 6
BF = ml_dtypes.bfloat16
def gentries(a):
    return np.ascontiguousarray(a.reshape(8, 16, -1).transpose(0, 2, 1)).reshape(8, -1)
def gtable(e):
    e = np.asarray(e); return np.ascontiguousarray(e.reshape(8, -1, 16).transpose(0, 2, 1)).reshape(128, -1).astype(np.int32)
W, C, S, F, HOPS, PH = 6144, 512, 6, 576, 2, 4
R = S * C
def lengths(rng, even):
    return 2 + rng.multinomial(W - F - 2 * C, rng.dirichlet(np.full(C, even)))
def short(rng):
    ln = 2 + (rng.random(C) < 0.3).astype(np.int64); ln[rng.integers(0, C)] += W - F - int(np.sum(ln)); return ln
def near(a, k):
    o, s, at, ln = a
    return o[s + (at + k) % ln]
def away(rng, a):
    return np.roll(near(a, rng.integers(0, W, (S, C))), C // 2, axis=1)
def store(rng, ln, o):
    s = F + np.concatenate([np.zeros(1, np.int64), np.add.accumulate(ln)[:-1]]); who = np.repeat(np.arange(C), ln)
    m = rng.integers(0, W, W); i = np.arange(F, W)
    m[o[F:]] = o[s[who] + (i - s[who] + 1) % ln[who]]
    return m, (o, s, np.minimum((rng.random(C) * ln).astype(np.int64), ln - 1), ln)
def put(o, i, v):
    j = int(np.flatnonzero(o == v)[0]); o[j] = o[i]; o[i] = v
def parts(rng, even=(0.5, 2.0, 20.0), share=0.6, ends=False):
    x = rng.integers(0, 16, (N, 8, 16, W), dtype=np.int32); q = rng.integers(0, 16, (N, 8, 16, R), dtype=np.int32); th = rng.integers(50, 90, (N, 8, R))
    nx = np.zeros((N, 8, W), np.int64); fr = np.zeros((N, 8, F), np.int64); cu = np.zeros((N, 8, C), np.int64); pin = np.zeros((N, 8, R), np.int64); a = {}
    for r in range(N):
        for g in range(8):
            o = rng.permutation(W)
            if ends and g % 4 == 0: put(o, 0, 0); put(o, F - 1, W - 1)
            if ends and g % 4 == 1: put(o, F, 0); put(o, F + 1, W - 1)
            if ends and g % 4 == 2: put(o, 0, W - 1); put(o, W - 1, 0)
            ln = short(rng) if ends else lengths(rng, float(rng.choice(np.array(even))))
            nx[r, g], s = store(rng, ln, o); a[r, g] = s
            fr[r, g] = o[:F]; cu[r, g] = near(s, 0)
            close = rng.random((S, C)) < share * rng.random((1, C))
            pin[r, g] = np.where(close, near(s, rng.integers(-5, 2, (S, C))), rng.integers(0, W, (S, C))).reshape(R)
    return x, nx, fr, cu, q, pin, th, a
def pack(x, nx, fr, cu, q, pin, th):
    return {"x": x.reshape(N, 128, W).astype(np.float32).astype(BF), "nx": nx.astype(np.int32), "fr": fr.astype(np.int32), "cu": np.stack([gtable(v) for v in cu]),
            "q": q.reshape(N, 128, R).astype(np.float32).astype(BF), "pin": np.stack([gtable(v) for v in pin]), "th": np.stack([gtable(v) for v in th])}
def setup_inputs(rng):
    x, nx, fr, cu, q, pin, th, a = parts(rng)
    return pack(x, nx, fr, cu, q, pin, th)
def setup_inputs_alike(rng):
    x, nx, fr, cu, q, pin, th, a = parts(rng)
    for r in range(N):
        for g in range(8):
            s = a[r, g]
            if g % 2 == 0:
                pin[r, g] = rng.choice(np.array([0, W - 1, near(s, 0)[0], near(s, 1)[1]]), R); q[r, g] = q[r, g][:, rng.integers(0, 2, R)]
            else:
                pin[r, g] = np.tile(np.roll(near(s, 0), -1), S); q[r, g] = np.tile(x[r, g][:, np.roll(near(s, 1), -1)], (1, S)); th[:, g] = 0
    return pack(x, nx, fr, cu, q, pin, th)
def setup_inputs_dry(rng):
    x, nx, fr, cu, q, pin, th, a = parts(rng)
    x[:, 4] = rng.integers(0, 16, (N, 16, 1))
    for g in (5, 6):
        x[:, g] = rng.integers(0, 2, (N, 16, 1)); q[:, g] = rng.integers(14, 16, (N, 16, R))
    m = min(C, F); L = F - m; d = C // 8
    for r in range(N):
        for g in range(8):
            s = a[r, g]; p = away(rng, s); T = np.full((S, C), 255); one = near(s, 1)
            if g in (0, 2):
                p = np.array(pin[r, g]).reshape(S, C); p[0] = near(s, 0); p[1] = near(s, 0); T = np.zeros((S, C), np.int64)
                q[r, g, :, :C] = x[r, g][:, one]; q[r, g, :, C:2 * C] = x[r, g][:, near(s, 2)]
            elif g == 4:
                p[0] = near(s, 0); w = rng.permutation(m); u = fr[r, g][rng.permutation(m)]; h = L + m // 2
                nx[r, g, u[:L]] = fr[r, g, m:]; nx[r, g, fr[r, g, m:]] = one[w[:L]]; p[1, w[:L]] = u[:L]; T[1, w[:L]] = 0
                nx[r, g, u[L:h]] = one[w[L:h]]; p[0, w[L:h]] = u[L:h]
            elif g == 5:
                e = m - d; b = L + d; k = int(rng.integers(1, 16)) if r % 2 == 0 else int(rng.integers(16, 48))
                p[0, :e] = near(s, 0)[:e]; T[0, :d] = 0; T[0, d:e] = 80; T[0, b + rng.permutation(e - b)[:k]] = 255
            elif g == 6:
                p[0] = one; T = rng.integers(150, 241, (S, C))
            pin[r, g] = p.reshape(R); th[(r + 1) % N, g] = T.reshape(R)
    return pack(x, nx, fr, cu, q, pin, th)
def setup_inputs_short(rng):
    x, nx, fr, cu, q, pin, th, a = parts(rng, ends=True); th = rng.integers(20, 130, (N, 8, R))
    for r in range(N):
        for g in range(8):
            s = a[r, g]; p = near(s, rng.integers(-2, 2, (S, C))).reshape(R)
            p = np.where(rng.random(R) < 0.25, fr[r, g][rng.integers(0, F, R)], p)
            pin[r, g] = np.where(rng.random(R) < 0.3, rng.integers(0, W, R), p)
            if g < 4: nx[r, g, fr[r, g]] = fr[r, g]
            if g == 7:
                e = np.flatnonzero((s[3] <= HOPS) & (rng.random(C) < 0.5)); v = near(s, 1)[e]; j = (C * np.arange(S)[:, None] + e[None, :]).reshape(-1)
                pin[r, g, j] = np.tile(v, S); q[r, g][:, j] = np.tile(x[r, g][:, v], (1, S)); th[(r + 1) % N, g, j] = 0
    return pack(x, nx, fr, cu, q, pin, th)
def setup_inputs_ties(rng):
    x, nx, fr, cu, q, pin, th, a = parts(rng, share=1.0)
    x[:, ::2] = rng.choice(np.array([2, 5, 6, 9]), (N, 4, 1, W)); q[:, ::2] = rng.integers(1, 11, (N, 4, 1, R)); th[:, ::2] = 16 * rng.integers(0, 5, (N, 4, R))
    x[:, 1::2] = rng.integers(0, 2, (N, 4, 16, W)); q[:, 1::2] = rng.integers(0, 2, (N, 4, 16, R)); th[:, 1::2] = rng.integers(2, 9, (N, 4, R))
    return pack(x, nx, fr, cu, q, pin, th)
def setup_inputs_spread(rng):
    x, nx, fr, cu, q, pin, th, a = parts(rng, even=(0.1, 0.3))
    x = np.minimum((16 * rng.random((N, 8, 16, W)) ** np.exp2(rng.integers(-2, 4, (N, 8, 1, W)))).astype(np.int32), 15)
    q = np.minimum((16 * rng.random((N, 8, 16, R)) ** np.exp2(rng.integers(-2, 4, (N, 8, 1, R)))).astype(np.int32), 15)
    return pack(x, nx, fr, cu, q, pin, rng.integers(0, 160, (N, 8, R)))
def check_inputs(d):
    bad = []
    for k in ("x", "q"):
        v = np.asarray(d[k]).astype(np.float32)
        if not np.all((v >= 0) & (v <= 15) & (v == np.floor(v))): bad.append("whole numbers of " + k)
    for k, hi in (("nx", W - 1), ("fr", W - 1), ("cu", W - 1), ("pin", W - 1), ("th", 255)):
        if np.min(d[k]) < 0 or np.max(d[k]) > hi: bad.append("range of " + k)
    if bad: return bad
    for r in range(N):
        cl = gentries(np.asarray(d["cu"][r])).astype(np.int64)
        for g in range(8):
            f = np.asarray(d["fr"][r][g]).astype(np.int64); m = np.asarray(d["nx"][r][g]).astype(np.int64)
            if len(np.unique(f)) != F:
                bad.append("different numbers of fr"); continue
            live = np.ones(W, bool); live[f] = False; ids = np.flatnonzero(live)
            if not np.array_equal(np.sort(m[ids]), ids) or np.any(m[ids] == ids):
                bad.append("rings of nx"); continue
            jump = np.where(live, m, np.arange(W)); lab = np.arange(W)
            for _ in range(W.bit_length()): lab = np.minimum(lab, lab[jump]); jump = jump[jump]
            if not np.all(live[cl[g]]) or not np.array_equal(np.sort(lab[cl[g]]), np.unique(lab[ids])): bad.append("one cursor in each ring")
    return sorted(set(bad))
def reference(x, nx, fr, cu, q, pin, th):
    X = x.astype(np.float32).astype(np.int32).reshape(N, 8, 16, W); Q = q.astype(np.float32).astype(np.int32).reshape(N, 8, 16, R); M = nx.astype(np.int64)
    c = np.stack([gentries(v) for v in cu]).astype(np.int64); P = np.stack([gentries(v) for v in pin]).astype(np.int64); t = np.stack([gentries(v) for v in th]).astype(np.int64)
    free = {(r, g): fr[r, g].astype(np.int64) for r in range(N) for g in range(8)}
    num = {k: np.zeros(0, np.int64) for k in free}; ring = {k: np.zeros(0, np.int64) for k in free}
    for phase in range(PH):
        n = P; old = P
        for h in range(HOPS):
            n = np.take_along_axis(M, n, 2); xn = np.take_along_axis(X, n[:, :, None, :], 3)
            d = np.add.reduce(np.abs(xn - Q), axis=2)
            if h == 0: least, at, xp = d, n, xn
            else:
                less = d < least
                least = np.where(less, d, least); at = np.where(less, n, at); xp = np.where(less[:, :, None, :], xn, xp)
        P = at; Q = (Q + xp) >> 1
        stay = np.roll(least >= t, -1, axis=0)
        for r, g in free:
            fl = free[r, g]; m = min(C, len(fl)); f = fl[:m]; a = c[r, g, :m].copy(); b = M[r, g, a]
            X[r, g][:, f] = (X[r, g][:, b] + X[r, g][:, a]) >> 1
            M[r, g, f] = M[r, g, b]; M[r, g, a] = f; c[r, g, :m] = f
            v = np.concatenate([num[r, g], b]); w = np.concatenate([ring[r, g], np.arange(m)])
            new4, old4, bit4 = P[r, g].reshape(S, C)[:, w], old[r, g].reshape(S, C)[:, w], stay[r, g].reshape(S, C)[:, w]
            held = np.any((new4 == v) | ((old4 == v) & bit4), axis=0)
            free[r, g] = np.concatenate([fl[m:], v[~held]]); num[r, g] = v[held]; ring[r, g] = w[held]
        if phase < PH - 1: Q = np.roll(Q, 1, axis=0)
    return {"yq": Q.reshape(N, 128, R).astype(np.float32).astype(BF), "yp": np.stack([gtable(v) for v in P]).astype(np.float32), "yn": M.astype(np.float32)}

from concourse.mybir import AluOpType as OP, ActivationFunctionType as AF

W, C, F, R, PH = 6144, 512, 576, 3072, 4
WW = W + C
BF, F32, I32, U16 = "bfloat16", "float32", "int32", "uint16"

CFG = {
    "cuts": [[0, 64, 128, 192]] * 4,
    "mode": [["rav", "rav", "rav"], ["rav", "rav", "aav"], ["rav", "rav", "aav"], ["rav", "aav", "rav"]],
    "wact": [0, 1, 1], "split": 0.375,
    "g": 1.56, "sc": 3.8, "f": 1.25, "pe": 0.00042, "link": 45.0, "hop": 0.1, "delta": 0.0, "dma": 250e3,
    "flip": [37, 39, 40, 42, 43, 44, 60, 73, 74, 75, 78, 86, 101, 104, 126, 151, 169, 182, 201, 206, 231, 254, 259, 284,
             286, 287, 324, 349, 401, 468, 493, 494],
    "order": [int(x) for x in """
22 21 24 20 27 23 19 25 30 12 0 4 6 1 7 8 16 13 17 14 18 15 5 3 2 9 31 32 36 66 33 57 51 48 34 35 55 65 63 47 59 56 79
58 70 129 49 41 39 52 46 44 40 67 104 80 81 60 69 50 53 11 105 71 86 106 87 130 111 72 54 43 42 74 73 88 131 64 37 82
112 94 89 90 158 92 113 83 132 159 136 91 93 84 85 137 95 10 160 114 45 61 62 96 172 76 115 107 161 97 108 98 138 99
162 100 117 118 116 109 119 110 120 139 140 142 121 134 184 141 143 122 101 123 133 124 77 75 185 144 135 145 209 146
186 125 191 68 147 126 154 102 103 155 127 29 164 210 148 165 192 211 78 149 157 167 216 26 150 193 234 163 169 199
217 156 235 173 194 151 174 175 170 197 176 195 187 177 236 178 188 166 171 179 128 198 196 152 38 244 180 218 181 182
183 189 190 200 245 266 219 267 237 212 201 269 268 213 202 270 203 272 271 204 246 273 205 153 220 221 214 222 223
215 224 225 226 247 240 238 241 239 242 250 168 251 248 249 274 243 227 206 252 253 228 275 229 254 207 208 230 302
303 327 277 255 262 256 231 257 304 265 258 328 278 309 352 310 263 264 329 276 279 311 284 283 281 288 334 289 290
291 292 353 285 293 259 305 294 317 335 286 295 287 354 296 306 297 298 336 312 300 362 28 232 233 260 315 313 307 308
299 314 316 319 337 318 363 355 330 320 301 321 331 322 364 323 332 338 340 384 333 339 341 342 343 261 385 280 356
387 386 388 324 344 390 389 345 391 392 401 346 393 365 358 357 360 359 282 366 368 367 361 369 370 371 372 373 347
374 380 348 375 325 326 418 443 397 381 382 349 419 420 444 376 383 350 396 425 402 426 398 403 404 405 406 407 408
427 421 399 409 410 445 411 433 412 471 377 422 428 431 472 453 413 414 415 473 416 351 423 424 454 429 432 400 446
430 447 434 455 417 497 435 478 498 378 379 394 395 474 500 499 436 501 437 502 475 503 456 448 479 449 450 480 438
451 461 452 457 459 481 458 482 504 439 505 460 463 462 464 465 466 467 468 440 483 484 485 441 476 477 486 487 488
507 506 508 489 490 491 496 492 493 494 469 509 442 511 470 510 495""".split()],
}

SCRATCH = {}
for _names, _cols, _dt in (
        ("X QA", WW, BF), ("AUX", WW + F, BF), ("L2 L3 QO0 QO1 QO2 QO3 YQ A1 A2 E1 E2 B1 B2 SD", R, BF),
        ("NXI", 384, I32), ("LHI", 768, I32), ("LH LH2", 768, BF), ("FRI", 40, I32), ("FHI", 80, I32), ("FH", 80, BF),
        ("YN Z", 384, F32), ("PINI THI KM PI", 192, I32), ("CUI", 32, I32), ("THB", 192, BF), ("CU0 NU", 32, U16),
        ("PU N1U N2U", 192, U16), ("K1", 192, F32), ("PF", 960, F32), ("PENS PENL", 576, BF), ("RET", 4 * C, BF),
        ("NN XC XN HP NEG", C, BF), ("NF OF", 96, F32), ("REP", 576, F32), ("ZU", 384, U16), ("TD", 64, F32),
        ("VB IB IN IK IR GM LT LO UP", 128, BF), ("EQ", 1152, BF), ("REL", 312, BF), ("CUM", 104, BF), ("OU", 96, U16),
        ("FL", 3 * F + 3 * C, BF), ("PCI", 8, I32), ("COL PCF", 8, F32), ("IU", 256, F32), ("IG IF", 128, F32),
        ("JT", 144, F32), ("RLF", 16, F32), ("RL", 16, U16), ("S1 SK SE SR", 144, BF), ("C25", 96, BF)):
    for _n in _names.split():
        SCRATCH[_n] = ("sbuf", [128, _cols], _dt)
for _k in range(8):
    SCRATCH["PS%d" % _k] = ("psum", [128, 512], F32)


def build(cfg):
    ops = []
    cyc = 0.00083 * cfg["f"]
    G, SC = cfg["g"], cfg["sc"]

    def ap(T, r):
        return T[r[0]][:, r[1]:r[2]]

    def add(eng, fn, rd, wr, cost, kind="c", **kw):
        o = {"id": len(ops), "eng": eng, "fn": fn, "rd": rd, "wr": wr, "cost": cost, "kind": kind, "after": []}
        o.update(kw)
        if o["id"] in cfg["flip"]:
            o["eng"], o["fn"], o["cost"], o["alt"] = o["alt"] + ((eng, fn, cost),)
        ops.append(o)
        return o

    def wide(r):
        return SCRATCH[r[0]][2] in (F32, I32)

    def vcost(n, c):
        return max(64, n * c) * cyc + 0.03

    def colr(s):
        return [s] if isinstance(s, tuple) else []

    def val(T, s):
        return ap(T, s) if isinstance(s, tuple) else s

    def vcopy(out, in_):
        c = 1 if wide(out) or wide(in_) else 0.5
        return add("v", lambda e, T: e.tensor_copy(ap(T, out), ap(T, in_)), [in_], [out], vcost(out[2] - out[1], c))

    def vts(out, in_, s1, o1, s2=None, o2=None):
        c = 1 if wide(out) or wide(in_) else 0.5
        if o2 is None:
            fn = lambda e, T: e.tensor_scalar(ap(T, out), ap(T, in_), val(T, s1), None, o1)
        else:
            fn = lambda e, T: e.tensor_scalar(ap(T, out), ap(T, in_), val(T, s1), val(T, s2), o1, o2)
        return add("v", fn, [in_] + colr(s1) + colr(s2), [out], vcost(out[2] - out[1], c))

    def vtt(out, a, b, o):
        c = 1 if a[0][:2] == "PS" or b[0][:2] == "PS" else 2
        return add("v", lambda e, T: e.tensor_tensor(ap(T, out), ap(T, a), ap(T, b), o), [a, b], [out],
                   vcost(out[2] - out[1], c))

    def vset(out, v):
        return add("v", lambda e, T: e.memset(ap(T, out), v), [], [out], vcost(out[2] - out[1], 1 if wide(out) else 0.5))

    def vgath(out, win, off, b, o):
        return add("v", lambda e, T: e.tensor_tensor(ap(T, out), ap(T, win).indirect(ap(T, off)), ap(T, b), o),
                   [win, off, b], [out], 0.05 + (out[2] - out[1]) * G * cyc)

    def vscat(win, off, a, b=None):
        if b is None:
            fn = lambda e, T: e.tensor_copy(ap(T, win).indirect(ap(T, off)), ap(T, a))
        else:
            fn = lambda e, T: e.tensor_tensor(ap(T, win).indirect(ap(T, off)), ap(T, a), ap(T, b), OP.add)
        return add("v", fn, [off, a] + colr(b), [win], 0.05 + (a[2] - a[1]) * SC * cyc)

    def act(out, in_, func, bias=0.0, scale=1.0):
        kw = {}
        if func != AF.Abs:
            s1, s2, o1, o2 = (bias, 0.0, OP.add, OP.max) if func == AF.Relu else (scale, bias, OP.mult, OP.add)
            kw["alt"] = ("v", lambda e, T: e.tensor_scalar(ap(T, out), ap(T, in_), val(T, s1), val(T, s2), o1, o2),
                         vcost(out[2] - out[1], 1 if wide(out) or wide(in_) else 0.5))
        return add("a", lambda e, T: e.activation(ap(T, out), ap(T, in_), func, bias=val(T, bias), scale=val(T, scale)),
                   [in_] + colr(bias) + colr(scale), [out], vcost(out[2] - out[1], 1) + 0.03, **kw)

    def agath(out, win, off):
        return add("a", lambda e, T: e.activation(ap(T, out), ap(T, win).indirect(ap(T, off)), AF.Copy),
                   [win, off], [out], 0.065 + (out[2] - out[1]) * G * cyc,
                   alt=("v", lambda e, T: e.tensor_copy(ap(T, out), ap(T, win).indirect(ap(T, off))),
                        0.05 + (out[2] - out[1]) * G * cyc))

    def pe(groups, opens=True, closes=True):
        rd, wr, cost = [], [], 0.06
        for out, mm in groups:
            wr.append(out)
            for l, r, s in mm:
                rd.extend([l, r])
                cost += max(64, out[2] - out[1]) * (4 if wide(l) else 1) * cfg["pe"] * cfg["f"]

        def fn(e, T):
            h = None
            for out, mm in groups:
                for k, (l, r, s) in enumerate(mm):
                    h = e.matmul(ap(T, out), ap(T, l), T[r[0]][:, r[1]:r[2]:s] if s > 1 else ap(T, r),
                                 opens and k == 0, closes and k == len(mm) - 1)
            return h
        return add("t", fn, rd, wr, cost)

    def tolist(sel, row):
        return [((sel, 15 - i, 143 - i), (row[0], row[1] + i, row[2]), 16) for i in range(16)]

    def iota(out, pat, base, cm):
        if SCRATCH[out[0]][2] == I32:
            fn = lambda e, T: e.iota(ap(T, out), pat, base, cm)
        else:
            fn = lambda e, T: e.iota(ap(T, out), pat, base, cm, allow_small_or_imprecise_dtypes=True)
        return add("g", fn, [], [out], 0.13 + 2 * cyc * (out[2] - out[1]))

    def dma(o, i, rd, wr, nbytes, q="s"):
        return add(q, lambda e, T: e.dma_start(o(T), i(T)), rd, wr, 0.1, kind="d", nbytes=nbytes)

    def load(dst, src, nbytes):
        return dma(lambda T: ap(T, dst), src, [], [dst], nbytes)

    def send(src, dst, back, name):
        nb = (src[2] - src[1]) * 256
        via = 0 if back else int((src[2] - src[1]) * cfg["split"]) // 16 * 16
        s = add("g", None, [src], [], 0.6 if via else 0.3, kind="s", src=src, dst=dst, back=back, name=name,
                nbytes=nb - via * 256, via=via)
        add("r", None, [], [dst], 0.0, kind="r", name=name, sender=s["id"], back=back)

    def rows(buf, i, a, b):
        return lambda T: T[buf][i::16, a:b]

    IB, IN, IK, IR, IF = [(n, 0, 128) for n in ("IB", "IN", "IK", "IR", "IF")]
    Xw, Aw = ("X", 0, W), ("AUX", 0, W)
    WB, HB = "PS6", "PS7"
    relu = "r" in "".join("".join(m) for m in cfg["mode"])

    load(("NXI", 0, 384), lambda T: T.nx[:], 196608)
    load(("PINI", 0, 192), lambda T: T.pin[:], 98304)
    for a in range(0, W, 1536):
        load(("X", a, a + 1536), lambda T, a=a: T.x[:, a:a + 1536], 393216)
    load(("CUI", 0, 32), lambda T: T.cu[:], 16384)
    load(("FRI", 0, 36), lambda T: T.fr[:], 18432)
    load(("THI", 0, 192), lambda T: T.th[:], 98304)
    for k in range(len(cfg["cuts"][0]) - 1):
        a, b = 16 * cfg["cuts"][0][k], 16 * cfg["cuts"][0][k + 1]
        load(("QA", a, b), lambda T, a=a, b=b: T.q[:, a:b], 256 * (b - a))
    vset(Aw, 0.0)
    for i, bits in ((0, 255), (1, 7936)):
        vts(("LHI", 384 * i, 384 * i + 384), ("NXI", 0, 384), bits, OP.bitwise_and)
        vcopy(("LH", 384 * i, 384 * i + 384), ("LHI", 384 * i, 384 * i + 384))
        dma(rows("AUX", i, 0, W), lambda T, i=i: T.LH[:, 384 * i:384 * i + 384], [("LH", 384 * i, 384 * i + 384)],
            [("AUX", 0, W, i)], 98304)
    iota(("PCI", 0, 1), [[0, 1]], 0, 1)
    iota(("IU", 0, 256), [[1, 256]], 0, 0)
    iota(("PCF", 0, 1), [[0, 1]], 0, 1)
    iota(("IG", 0, 128), [[16, 8], [0, 16]], 0, 0)
    iota(("JT", 0, 144), [[16, 144]], -4096, 0)
    iota(("RLF", 0, 12), [[0, 6], [16, 2]], 0, 0)
    iota(("AUX", W, WW + F), [[0, C + F]], 0, 0)
    iota(("FL", 3 * F, 3 * F + 3 * C), [[0, 3 * C]], 0, 0)
    iota(("X", W, WW), [[0, C]], 0, 0)
    iota(("QA", W, WW), [[0, C]], 0, 0)
    iota(("NEG", 0, C), [[0, C]], -160, 0)
    iota(("VB", 0, 32), [[0, 32]], 1, 0)
    vts(("PCI", 2, 3), ("PCI", 0, 1), 112, OP.bitwise_and)
    vts(("PCI", 3, 4), ("PCI", 0, 1), 15, OP.bitwise_and)
    vcopy(("COL", 0, 2), ("PCI", 2, 4))
    g16, ic, g15, m0, m24, m25, pc = [("COL", k, k + 1) for k in range(6)] + [("PCF", 0, 1)]
    vts(g15, g16, 15.0, OP.add)
    vts(("S1", 0, 144), ("IU", 0, 144), g15, OP.is_equal)
    vcopy(("PU", 0, 192), ("PINI", 0, 192))
    act(("SK", 0, 144), ("S1", 0, 144), AF.Identity, 0.0, 16384.0)
    if relu:
        iota(("C25", 0, 96), [[0, 96]], -2560, 0)
        act(("SE", 0, 144), ("S1", 0, 144), AF.Identity, 0.0, -16384.0)
        act(("SR", 0, 144), ("S1", 0, 144), AF.Identity, 0.0, 32768.0)
    vts(IB, ("IU", 0, 128), pc, OP.is_equal)
    for t, w in ((IN, -1.0), (IK, 16384.0), (IR, -4096.0), (IF, 1.0)):
        act(t, IB, AF.Identity, 0.0, w)
    vts(("THB", 0, 192), ("THI", 0, 192), -1.0, OP.mult, 256.0, OP.add)
    vcopy(("CU0", 0, 32), ("CUI", 0, 32))
    for i, bits in ((0, 255), (1, 7936)):
        vts(("FHI", 40 * i, 40 * i + 36), ("FRI", 0, 36), bits, OP.bitwise_and)
        vcopy(("FH", 40 * i, 40 * i + 36), ("FHI", 40 * i, 40 * i + 36))
        dma(rows("AUX", i, WW, WW + F), lambda T, i=i: T.FH[:, 40 * i:40 * i + 36], [("FH", 40 * i, 40 * i + 40)],
            [("AUX", WW, WW + F, i)], 9216)
    vcopy(("PF", 0, 192), ("PINI", 0, 192))
    vts(m0, ic, 0.0, OP.is_equal)
    vts(m24, ic, 1.0, OP.is_equal, 6144.0, OP.mult)
    vts(m25, ic, 1.0, OP.is_equal, 6400.0, OP.mult)
    act(("FL", 0, 256), ("IU", 0, 256), AF.Identity, m24, m0)
    act(("FL", 256, 512), ("IU", 0, 256), AF.Identity, m25, m0)
    act(("FL", 512, 576), ("IU", 0, 64), AF.Identity, m24, m0)
    for k in (1, 2):
        dma(lambda T, k=k: T.FL[:, k * F:k * F + F], lambda T: T.FL[:, 0:F], [("FL", 0, F)], [("FL", k * F, k * F + F)], 147456)
    vts(("JT", 0, 144), ("JT", 0, 144), ic, OP.add)
    vts(("RL", 0, 12), ("RLF", 0, 12), ic, OP.add)
    vts(("GM", 0, 128), ("IG", 0, 128), g16, OP.is_equal)
    vts(("LT", 0, 128), ("IU", 0, 128), pc, OP.is_gt)
    vtt(("LO", 0, 128), ("GM", 0, 128), ("LT", 0, 128), OP.mult)
    vtt(("UP", 0, 128), ("GM", 0, 128), ("LO", 0, 128), OP.subtract)
    act(("REL", 1, 2), m0, AF.Identity, 0.0, 64.0)

    qin = [("QA", 0), ("QA", R), ("L2", 0), ("L3", 0)]
    fl = [("AUX", WW), ("FL", 0), ("FL", F), ("FL", 2 * F)]
    turn = [0]

    def through_psum(out, xg, q, sign, func, bias, scale):
        for s in range(0, out[2] - out[1], 512):
            n = min(512, out[2] - out[1] - s)
            ps = ("PS%d" % (4 + turn[0] % 2), 0, n)
            turn[0] += 1
            pe([(ps, [(IB, (xg[0], xg[1] + s, xg[1] + s + n), 1), (sign, (q[0], q[1] + s, q[1] + s + n), 1)])])
            act((out[0], out[1] + s, out[1] + s + n), ps, func, bias, scale)

    def cursors(p):
        return ("CU0", 0, 32) if p == 0 else (("ZU", 0, 32) if p == 1 else ("ZU", 96 * p - 32, 96 * p))

    def prepare(p):
        cu = cursors(p)
        ret = ("RET", C * p, C * p + C)
        nn = ("RET", C, 2 * C) if p == 0 else ("NN", 0, C)
        if p != 1:
            agath(ret, Aw, cu)
        pe([((WB, 0, 32), tolist("S1", ret))])
        vcopy(("NU", 0, 32), (WB, 0, 32))
        agath(nn, Aw, ("NU", 0, 32))
        if p < 3:
            act(("NF", 32 * p, 32 * p + 32), (WB, 0, 32), AF.Copy)
            agath(("REP", 192 * p, 192 * p + 192), ("NF", 32 * p, 32 * p + 32), ("RL", 0, 12))
            xc, hb = (("HP", 0, C), 79.75) if p == 1 else (("XC", 0, C), 159.75)
            if p != 1:
                agath(xc, Xw, cu)
            if cfg["wact"][p]:
                agath(("XN", 0, C), Xw, ("NU", 0, 32))
                pe([((WB, 0, C), [(IB, xc, 1), (IB, ("XN", 0, C), 1)])])
                act(("HP", 0, C), (WB, 0, C), AF.Identity, hb, 0.5)
            else:
                vgath(("XN", 0, C), Xw, ("NU", 0, 32), xc, OP.add)
                act(("HP", 0, C), ("XN", 0, C), AF.Identity, hb, 0.5)

    prepare(0)
    for p in range(PH):
        off = 160.0 if p else 0.0
        cu = cursors(p)
        cf = None if p == 0 else (("Z", 0, 32) if p == 1 else ("Z", 96 * p - 32, 96 * p))
        cuts = cfg["cuts"][p]
        nn = ("RET", C, 2 * C) if p == 0 else ("NN", 0, C)
        for k in range(len(cuts) - 1):
            c0, c1 = cuts[k], cuts[k + 1]
            a, b = 16 * c0, 16 * c1
            mode = cfg["mode"][p][k]
            q = (qin[p][0], qin[p][1] + a, qin[p][1] + b)
            src = ("PU", c0, c1)
            for h in (1, 2):
                ps, pk = ("PS%d" % (h - 1), 0, c1 - c0), ("PS%d" % (h + 1), 0, c1 - c0)
                row, nu, e, ab = ("A%d" % h, a, b), ("N%dU" % h, c0, c1), ("E%d" % h, a, b), ("B%d" % h, a, b)
                agath(row, Aw, src)
                pe([(ps, tolist("S1", row))])
                vcopy(nu, ps)
                mm = [(IK, ("THB", c0, c1), 1)]
                if mode[h - 1] == "a":
                    agath(e, Xw, nu)
                    through_psum(ab, e, q, IN, AF.Abs, off, 1.0)
                elif mode[h - 1] == "v":
                    vgath(e, Xw, nu, q, OP.subtract)
                    act(ab, e, AF.Abs, off)
                else:
                    vgath(e, Xw, nu, q, OP.subtract)
                    vts(ab, e, off, OP.add, 0.0, OP.max)
                    mm += ([(IK, ("C25", 0, c1 - c0), 1)] if p else []) + tolist("SE", e)
                pe([(pk, mm + tolist("S1", row))], closes=False)
                pe([(pk, tolist("SR" if mode[h - 1] == "r" else "SK", ab))], opens=False)
                src = nu
            act(("K1", c0, c1), ("PS2", 0, c1 - c0), AF.Identity, -8192.0)
            vtt(("KM", c0, c1), ("PS3", 0, c1 - c0), ("K1", c0, c1), OP.min)
            vts(("PI", c0, c1), ("KM", c0, c1), 8191, OP.bitwise_and)
            vcopy(("PU", c0, c1), ("PI", c0, c1))
            qo = ("QO%d" % p, a, b)
            if mode[2] == "a":
                agath(("SD", a, b), Xw, ("PU", c0, c1))
                through_psum(qo, ("SD", a, b), q, IB, AF.Identity, 159.75 - off / 2, 0.5)
            else:
                vgath(("SD", a, b), Xw, ("PU", c0, c1), q, OP.add)
                act(qo, ("SD", a, b), AF.Identity, 159.75 - off / 2, 0.5)
            if p < 3:
                send(qo, (qin[p + 1][0], qin[p + 1][1] + a, qin[p + 1][1] + b), False, "q%d_%d" % (p, k))
            else:
                act(("YQ", a, b), qo, AF.Identity, -160.0)
                dma(lambda T, a=a, b=b: T.yq[:, a:b], lambda T, a=a, b=b: T.YQ[:, a:b], [("YQ", a, b)], [], 256 * (b - a))
        pn, po = ("PF", 192 * p + 192, 192 * p + 384), ("PF", 192 * p, 192 * p + 192)
        if p < 3:
            pen = ("PENS", 192 * p, 192 * p + 192)
            vts(pen, ("KM", 0, 192), 4186112.0, OP.is_lt, 8192.0, OP.mult)
            send(pen, ("PENL", 192 * p, 192 * p + 192), True, "b%d" % p)
        vcopy(pn, ("PI", 0, 192))
        flp = (fl[p][0], fl[p][1], fl[p][1] + C)
        z = 96 * p
        pe([((WB, 32, 64), tolist("S1", flp))])
        if p == 0:
            vcopy(("ZU", 0, 32), (WB, 32, 64))
            act(("Z", 0, 32), (WB, 32, 64), AF.Copy)
            ct = cu
        else:
            ff, v = ("Z", z, z + 32), ("VB", 32 * p, 32 * p + 32)
            act(ff, (WB, 32, 64), AF.Copy)
            vts(v, ff, 6144.0, OP.is_lt)
            vtt(("TD", 0, 32), cf, ff, OP.subtract)
            vtt(("TD", 32, 64), ("TD", 0, 32), v, OP.mult)
            vtt(("Z", z + 32, z + 64), ff, ("TD", 32, 64), OP.add)
            if p < 3:
                vtt(("Z", z + 64, z + 96), cf, ("TD", 32, 64), OP.subtract)
            n = 96 if p < 3 else 64
            vcopy(("ZU", z, z + n), ("Z", z, z + n))
            ct = ("ZU", z + 32, z + 64)
        tab = ("AUX" if p < 3 else "QA", 0, WW)
        vscat(tab, ("ZU", z, z + 32), nn)
        vscat(tab, ct, flp)
        if p == 2:
            for i in (0, 1):
                dma(rows("QA", i, 0, W), rows("AUX", i, 0, W), [Aw], [("QA", 0, W, i)], 98304)
        if p == 3:
            for i in (0, 1):
                dma(lambda T, i=i: T.LH2[:, 384 * i:384 * i + 384], rows("QA", i, 0, W), [("QA", 0, W)],
                    [("LH2", 384 * i, 384 * i + 384)], 98304)
            pe([((HB, 0, 384), [(IB, ("LH2", 0, 384), 1), (IB, ("LH2", 384, 768), 1)])])
            act(("YN", 0, 384), (HB, 0, 384), AF.Copy)
            dma(lambda T: T.yn[:], lambda T: T.YN[:], [("YN", 0, 384)], [], 196608)
            dma(lambda T: T.yp[:], lambda T: T.PF[:, 768:960], [pn], [], 98304)
            break
        vscat(("X", 0, WW), ("ZU", z, z + 32), ("HP", 0, C), ("NEG", 0, C))
        prepare(p + 1)
        n = 32 * (p + 1)
        r0 = 104 * p
        act((fl[p + 1][0], fl[p + 1][1], fl[p + 1][1] + 64), (fl[p][0], fl[p][1] + C, fl[p][1] + F), AF.Copy)
        pe([((HB, 0, 192), [(IF, pn, 1)]),
            ((HB, 192, 384), [(IF, po, 1), (IB, ("PENL", 192 * p, 192 * p + 192), 1)])])
        for blk in range(p + 1):
            for s in (0, 192):
                vtt(("EQ", 384 * blk + s, 384 * blk + s + 192), (HB, s, s + 192), ("REP", 192 * blk, 192 * blk + 192), OP.is_equal)
        pe([((HB, 384 + 32 * blk, 416 + 32 * blk),
             [(IB, ("EQ", 384 * blk + 32 * s, 384 * blk + 32 * s + 32), 1) for s in range(12)]
             + [(IN, ("VB", 32 * blk, 32 * blk + 32), 1)]
             + [(IB, ("REL", 104 * pp + 2 + 32 * blk, 104 * pp + 34 + 32 * blk), 1) for pp in range(blk, p)])
            for blk in range(p + 1)])
        rel = ("REL", r0 + 2, r0 + 2 + n)
        vts(rel, (HB, 384, 384 + n), -1.0, OP.is_equal)
        lead, cum = ("REL", r0 + 1, r0 + 2 + n), ("CUM", 1, 2 + n)
        add("v", lambda e, T, lead=lead, cum=cum: e.tensor_tensor_scan(ap(T, cum), ap(T, lead), ap(T, lead), 0.0, OP.add, OP.max),
            [lead], [cum], vcost(n + 1, 1))
        grp = [((WB, 64, 64 + n), [(("LO", 0, 128), ("CUM", 2, 2 + n), 1), (("UP", 0, 128), ("CUM", 1, 1 + n), 1), (IR, rel, 1)])]
        if p < 2:
            grp.append(((WB, 160, 161), [(("S1", 15, 143), ("CUM", 1 + n, 2 + n), 1)]))
        pe(grp)
        d0 = (3 - p) * F // 16
        vtt(("OF", 0, n), (WB, 64, 64 + n), ("JT", d0, d0 + n), OP.min)
        vts(("OU", 0, n), ("OF", 0, n), 4096.0, OP.add)
        if p < 2:
            act(("REL", r0 + 105, r0 + 106), (WB, 160, 161), AF.Relu, -512.0)
        for blk in range(p + 1):
            vscat(("FL", p * F, 3 * F + 3 * C), ("OU", 32 * blk, 32 * blk + 32), ("RET", C * blk, C * blk + C))
    return ops


def hazards(ops):
    seen = {}
    for o in ops:
        deps, same = set(), set()
        acc = [(r, False) for r in o["rd"]] + [(r, True) for r in o["wr"]]
        for r, w in set(acc):
            ps = r[0][:2] == "PS"
            for (j, r2, w2) in seen.get(r[0], []):
                if ps:
                    (deps if ops[j]["eng"] != o["eng"] or "alt" in o or "alt" in ops[j] else same).add(j)
                elif (w or w2) and r[1] < r2[2] and r2[1] < r[2] and not (len(r) > 3 and len(r2) > 3 and r[3] != r2[3]):
                    deps.add(j)
        for r, w in set(acc):
            seen.setdefault(r[0], []).append((o["id"], r, w))
        if o["kind"] == "r":
            deps, same = set(), {o["sender"]}
        o["deps"] = sorted(deps)
        o["pre"] = sorted(deps | same | set(o["after"]))


def plan(cfg):
    ops = build(cfg)
    hazards(ops)
    order = cfg["order"]
    pos = {i: k for k, i in enumerate(order)}
    assert len(pos) == len(ops) and all(pos[j] < pos[o["id"]] for o in ops for j in o["pre"])
    count = {"v": 0, "a": 0, "t": 0, "g": 0}
    sems = ["cv", "ca", "ct", "cg", "sent"]
    know = {e: {} for e in "vatgs"}
    for i in order:
        o = ops[i]
        if o["kind"] == "r":
            o["sem"], o["n"], o["know"] = "r" + o["name"], 1, {}
            sems.append(o["sem"])
            continue
        kn = know[o["eng"]]
        o["waits"] = []
        for j in sorted(o["deps"], key=lambda j: -pos[j]):
            d = ops[j]
            if d["kind"] == "s" or kn.get(d["sem"], 0) >= d["n"]:
                continue
            o["waits"].append(j)
            kn[d["sem"]] = d["n"]
            for s, v in d["know"].items():
                kn[s] = max(kn.get(s, 0), v)
        o["know"] = dict(kn)
        if o["kind"] == "s" and o["via"]:
            sems.append("h" + o["name"])
        if o["kind"] == "d":
            o["sem"], o["n"] = "d%d" % i, 16
            sems.append(o["sem"])
        elif o["kind"] == "c":
            count[o["eng"]] += 1
            o["sem"], o["n"] = "c" + o["eng"], count[o["eng"]]
    return ops, order, sems, count


OPS, ORDER, SEMAPHORES, COUNT = plan(CFG)


def helper_of(core, to, T, topo):
    return [c for c in topo.cores_of(core)
            if topo.die(c) != topo.die(core) and topo.may_write(c, to) and T.rank_of(c) is None][0]


def spare(core, helper, to, topo):
    return [e for e in topo.engines(core, helper) if e not in topo.engines(core, to)]


def write(g, T, src, dst, sem, to, engines, topo):
    rid, pid, _ = topo.addr(to)
    g.remote_dma(T[dst[0]][:, dst[1]:dst[2]], T[src[0]][:, src[1]:src[2]], T.sem[sem], T.sem["sent"], pid, rid,
                 sum(1 << e for e in engines))
    return len(engines)


def rank_program(g, core, T, topo):
    rank = T.rank_of(core)
    n = len(T.cores)
    sent = 0
    if rank is None:
        for r in range(n):
            own, to = T.cores[r], T.cores[(r + 1) % n]
            if helper_of(own, to, T, topo) == core:
                for i in ORDER:
                    o = OPS[i]
                    if o["kind"] == "s" and o["via"]:
                        part = (o["dst"][0], o["dst"][2] - o["via"], o["dst"][2])
                        g.wait_ge(T.sem["h" + o["name"]], len(spare(own, core, to, topo)))
                        sent += write(g, T, part, part, "r" + o["name"], to, topo.engines(core, to), topo)
                if sent:
                    g.wait_ge(T.sem["sent"], sent)
        return
    nxt, prv = T.cores[(rank + 1) % n], T.cores[(rank - 1) % n]
    queue = {"v": g.vector, "a": g.scalar, "t": g.tensor, "g": g, "s": g.sync}

    def target(d):
        if d["kind"] != "r":
            return d["n"]
        k = len(topo.engines(nxt if d["back"] else prv, core))
        if OPS[d["sender"]]["via"]:
            k += len(topo.engines(helper_of(prv, core, T, topo), core))
        return k
    for i in ORDER:
        o = OPS[i]
        if o["kind"] == "r":
            continue
        e = queue[o["eng"]]
        for j in o["waits"]:
            e.wait_ge(T.sem[OPS[j]["sem"]], target(OPS[j]))
        if o["kind"] == "s":
            to = prv if o["back"] else nxt
            s, d, v = o["src"], o["dst"], o["via"]
            if v:
                h = helper_of(core, to, T, topo)
                sent += write(g, T, (s[0], s[2] - v, s[2]), (d[0], d[2] - v, d[2]), "h" + o["name"], h,
                              spare(core, h, to, topo), topo)
            sent += write(g, T, (s[0], s[1], s[2] - v), (d[0], d[1], d[2] - v), "r" + o["name"], to,
                          topo.engines(core, to), topo)
        else:
            o["fn"](e, T).then_inc(T.sem[o["sem"]], 16 if o["kind"] == "d" else 1)
    for k in ("g", "t", "a", "v"):
        g.wait_ge(T.sem["c" + k], COUNT[k])
    g.wait_ge(T.sem["sent"], sent)
    for i in ORDER:
        if OPS[i]["kind"] in "rd":
            g.wait_ge(T.sem[OPS[i]["sem"]], target(OPS[i]))
